import numpy as np
import ml_dtypes


def mxq(x, axis, fmt="e4m3"):
    dtype, down = {"e4m3": (ml_dtypes.float8_e4m3fn, 7), "e5m2": (ml_dtypes.float8_e5m2, 14)}[fmt]
    v = np.moveaxis(np.asarray(x, np.float32).astype(ml_dtypes.bfloat16).astype(np.float64), axis, -1)
    blocks = v.reshape(v.shape[:-1] + (-1, 32))
    amax = np.abs(blocks).max(-1, keepdims=True)
    byte = np.maximum(np.where(amax > 0, np.frexp(amax)[1] - 1 + 127, 0) - down, 1)
    scale = np.exp2(byte - 127.0)
    codes = (blocks / scale).astype(np.float32).astype(dtype).astype(np.float64)
    return np.moveaxis((codes * scale).reshape(v.shape), -1, axis)


WIDE = False


def mx_kscale(k, group=512):
    if not WIDE:
        return np.ones(k)
    levels = np.array([18, -18])
    if group != 512:
        return np.exp2(np.random.permutation(np.resize(levels, k // group))).repeat(group)
    if k % 512:
        return np.exp2(np.random.permutation(np.resize(levels, k // 32))).repeat(32)
    a = np.empty((k // 512, 16))
    for p in range(k // 512):
        a[p, :8] = np.random.permutation(np.resize(levels, 8))
        for g in range(8):
            far = levels[np.abs(levels - a[p, g]) >= 10]
            a[p, g + 8] = far[np.random.randint(len(far))]
    return np.exp2(a.ravel()).repeat(32)


def f64(x):
    return np.asarray(x).astype(np.float64)


E2M1 = np.array([0.0, 0.5, 1.0, 1.5, 2.0, 3.0, 4.0, 6.0, -0.0, -0.5, -1.0, -1.5, -2.0, -3.0, -4.0, -6.0])


def pack_group(w):
    k, n = w.shape
    w = f64(np.asarray(w, np.float32).astype(ml_dtypes.bfloat16)).reshape(k // 32, 32, n)
    amax = np.abs(w).max(1)
    mant, ex = np.frexp(amax / 6.0)
    byte = np.clip(np.where(amax > 0, np.where(mant > 0.5, ex, ex - 1) + 127, 1), 1, 254)
    scaled = (w * np.exp2(127.0 - byte)[:, None, :]).reshape(k, n).astype(np.float32)
    c = np.ascontiguousarray(scaled.reshape(k // 4, 4, n).transpose(0, 2, 1)).astype(ml_dtypes.float4_e2m1fn).view(np.uint8) & 0xF
    return np.ascontiguousarray((c[..., 0::2] | (c[..., 1::2] << 4)).reshape(k // 4, 2 * n)), byte.astype(np.uint8)


def unpack_group(words, scales):
    p, n = words.shape[0], scales.shape[1]
    words = np.ascontiguousarray(words).reshape(p, n, 2)
    nib = np.empty((p, n, 4), np.uint8)
    nib[..., 0::2] = words & 0xF
    nib[..., 1::2] = words >> 4
    return E2M1[nib].transpose(0, 2, 1).reshape(4 * p, n) * np.repeat(np.exp2(scales.astype(np.float64) - 127.0), 32, axis=0)


def silu(v):
    return v / (1.0 + np.exp(-v))


def bf(x):
    return np.asarray(x, np.float32).astype(ml_dtypes.bfloat16)


def planes(Y):
    r, m = Y.shape
    b = f64(bf(Y)).reshape(r // 32, 32, m)
    amax = np.abs(b).max(1)
    byte = np.clip(np.where(amax > 0, np.frexp(amax)[1] - 1 + 127 - 7, 1), 1, 254)
    codes = (b * np.exp2(127.0 - byte)[:, None, :]).reshape(r, m).astype(np.float32).astype(ml_dtypes.float8_e4m3fn).view(np.uint8)
    words = codes.reshape(r // 512, 128, 4, m).transpose(0, 1, 3, 2)
    return np.ascontiguousarray(words), np.ascontiguousarray(byte.astype(np.uint8).reshape(r // 512, 16, m))


G, D, M, N = 4, 128, 128, 512


def setup_inputs():
    n = np.random.standard_normal
    s_d = mx_kscale(D, 0)
    w_ = [pack_group(w) for w in n((G, D, M)) / np.sqrt(D) / s_d[:, None]]
    u_ = [pack_group(w) for w in n((G, D, M)) / np.sqrt(D) / s_d[:, None]]
    return {
        "x": (n((G, D, N)) * s_d[:, None]).astype(np.float32),
        "w_words": np.stack([w[0] for w in w_]),
        "w_scales": np.stack([w[1] for w in w_]),
        "u_words": np.stack([w[0] for w in u_]),
        "u_scales": np.stack([w[1] for w in u_]),
    }


def reference(x, w_words, w_scales, u_words, u_scales):
    w = np.stack([unpack_group(w_words[g], w_scales[g]) for g in range(G)])
    xq = mxq(f64(x), 1, "e4m3")
    zw = w.transpose(0, 2, 1) @ xq
    u = np.stack([unpack_group(u_words[g], u_scales[g]) for g in range(G)])
    zu = u.transpose(0, 2, 1) @ xq
    y = silu(zw) * zu
    Y = y.reshape(G * M, N)
    words, scales = planes(Y)
    return Y, words, scales

@@ -1,0 +1,125 @@
+from contextlib import ExitStack
+
+import concourse.mybir as mybir
+
+G, D, M, N = 4, 128, 128, 512
+FLOPS = 2 * 2 * G * D * M * N
+
+F32 = mybir.dt.float32
+BF16 = mybir.dt.bfloat16
+I32 = mybir.dt.int32
+U32 = mybir.dt.uint32
+U8 = mybir.dt.uint8
+FP8X4 = mybir.dt.float8_e4m3fn_x4
+FP4X4 = mybir.dt.float4_e2m1fn_x4
+ACT = mybir.ActivationFunctionType
+ALU = mybir.AluOpType
+
+P = 128
+PACK = 4
+ROWS = D // PACK
+HALF = N // 2
+ORDER = (0, 2, 1, 3)
+SPLIT = 160
+
+
+def interleave(copy, dst, src, c0, c1):
+    copy(
+        out=dst[:, c0:c1, :].rearrange("p (c i) t -> p c t i", i=4),
+        in_=src[:, :, c0:c1].rearrange("p t (c i) -> p c t i", i=4),
+    )
+
+
+def quantise(nc, codes, scales, grouped):
+    nc.vector.quantize_mx(
+        out=codes.bitcast(FP8X4), scales=scales, in_=grouped[:].rearrange("p n t -> p (n t)")
+    )
+
+
+def tile_rows_pl_gswiglu4_kernel(tc, x, w_words, w_scales, u_words, u_scales, out_0, out_1, out_2):
+    nc = tc.nc
+    with ExitStack() as ctx:
+        sb = ctx.enter_context(tc.tile_pool(name="sb", bufs=1))
+        ps = ctx.enter_context(tc.psum_pool(name="ps", bufs=1))
+        ctx.enter_context(tc.manual_schedule())
+
+        halves = [slice(h * HALF, (h + 1) * HALF) for h in range(2)]
+        x_rows = x.rearrange("g (p j) n -> (g p) j n", j=PACK)
+        x_raw = [sb.tile([P, PACK, HALF], F32, name="x_raw%d" % h, align_bytes=64) for h in range(2)]
+        x_grp = [sb.tile([P, HALF, PACK], BF16, name="x_grp%d" % h, align_bytes=64) for h in range(2)]
+        x_codes = sb.tile([P, N], U32, name="x_codes", align_bytes=64)
+        x_scales = sb.tile([P, N], U8, name="x_scales", align_bytes=64)
+        words = [sb.tile([P, 2 * M], U8, name="words%d" % i, align_bytes=64) for i in range(2)]
+        planes = [sb.tile([P, M], U8, name="planes%d" % i, align_bytes=64) for i in range(2)]
+        gate = sb.tile([P, G, N], F32, name="gate", align_bytes=64)
+        y = sb.tile([P, G, N], F32, name="y", align_bytes=64)
+        y_raw = [sb.tile([P, PACK, HALF], F32, name="y_raw%d" % h, align_bytes=64) for h in range(2)]
+        y_grp = [sb.tile([P, HALF, PACK], BF16, name="y_grp%d" % h, align_bytes=64) for h in range(2)]
+        y_codes = [sb.tile([P, HALF], U32, name="y_codes%d" % h, align_bytes=64) for h in range(2)]
+        y_scales = sb.tile([P, N], U8, name="y_scales", align_bytes=64)
+        z = [[ps.tile([P, N], F32, name="z%d_%d" % (i, g)) for g in range(G)] for i in range(2)]
+
+        for i in range(2):
+            nc.vector.memset(planes[i][:].bitcast(U32), 0)
+
+        src_words = (w_words, u_words)
+        src_scales = (w_scales, u_scales)
+        for h in range(2):
+            nc.scalar.dma_start(
+                out=words[h][:].bitcast(I32), in_=src_words[h].rearrange("g p b -> (g p) b").bitcast(I32)
+            )
+            nc.sync.dma_start(out=x_raw[h][:], in_=x_rows[:, :, halves[h]])
+        for i, queue in enumerate((nc.scalar, nc.sync)):
+            for g in ORDER:
+                queue.dma_start(
+                    out=planes[i][ROWS * g : ROWS * g + 4, :].bitcast(I32), in_=src_scales[i][g].bitcast(I32)
+                )
+
+        for h in range(2):
+            interleave(nc.vector.tensor_copy, x_grp[h], x_raw[h], 0, HALF)
+            quantise(nc, x_codes[:, halves[h]], x_scales[:, halves[h]], x_grp[h])
+
+        for i in range(2):
+            for g in ORDER:
+                rows = slice(ROWS * g, ROWS * (g + 1))
+                nc.tensor.matmul_mx(
+                    out=z[i][g][:],
+                    lhsT=words[i][rows, :].bitcast(FP4X4),
+                    lhsT_scale=planes[i][rows, :],
+                    rhs=x_codes[rows, :].bitcast(FP8X4),
+                    rhs_scale=x_scales[rows, :],
+                    start=True,
+                    stop=True,
+                )
+
+        chunks = [(h, g) for h in range(2) for g in ORDER]
+
+        def regroup(k):
+            h, g = chunks[k]
+            queue = nc.sync if g < 2 else nc.scalar
+            queue.dma_start(out=y_raw[h][ROWS * g : ROWS * (g + 1), :, :], in_=y[:, g, halves[h]])
+
+        LAG = 2
+        for k, (h, g) in enumerate(chunks):
+            nc.scalar.activation(out=gate[:, g, halves[h]], in_=z[0][g][:, halves[h]], func=ACT.Silu)
+            nc.vector.tensor_tensor(
+                out=y[:, g, halves[h]], in0=z[1][g][:, halves[h]], in1=gate[:, g, halves[h]], op=ALU.mult
+            )
+            if k >= LAG:
+                regroup(k - LAG)
+        for k in range(len(chunks) - LAG, len(chunks)):
+            regroup(k)
+        nc.scalar.dma_start(out=out_0.rearrange("(g m) n -> m g n", g=G), in_=y[:])
+
+        out_words = out_1[0].rearrange("p n t -> p (n t)").bitcast(I32)
+        for h in range(2):
+            interleave(nc.vector.tensor_copy, y_grp[h], y_raw[h], 0, SPLIT)
+            interleave(nc.scalar.copy, y_grp[h], y_raw[h], SPLIT, HALF)
+            quantise(nc, y_codes[h][:], y_scales[:, halves[h]], y_grp[h])
+            nc.sync.dma_start(out=out_words[:, halves[h]], in_=y_codes[h][:].bitcast(I32))
+        for q in range(4):
+            queue = nc.scalar if q < 2 else nc.sync
+            queue.dma_start(
+                out=out_2[0, 4 * q : 4 * q + 4, :].bitcast(I32),
+                in_=y_scales[32 * q : 32 * q + 4, :].bitcast(I32),
+            )

@@ -20,7 +20,8 @@ PACK = 4
 ROWS = D // PACK
 HALF = N // 2
 ORDER = (0, 2, 1, 3)
-SPLIT = 160
+SPLIT = 192
+QUARTER = HALF // 2
 
 
 def interleave(copy, dst, src, c0, c1):
@@ -47,20 +48,23 @@ def tile_rows_pl_gswiglu4_kernel(tc, x, w_words, w_scales, u_words, u_scales, ou
         x_rows = x.rearrange("g (p j) n -> (g p) j n", j=PACK)
         x_raw = [sb.tile([P, PACK, HALF], F32, name="x_raw%d" % h, align_bytes=64) for h in range(2)]
         x_grp = [sb.tile([P, HALF, PACK], BF16, name="x_grp%d" % h, align_bytes=64) for h in range(2)]
-        x_codes = sb.tile([P, N], U32, name="x_codes", align_bytes=64)
-        x_scales = sb.tile([P, N], U8, name="x_scales", align_bytes=64)
+        x_codes = sb.tile([P, HALF + N], U32, name="x_codes", align_bytes=64)
+        x_scales = sb.tile([P, HALF + N], U8, name="x_scales", align_bytes=64)
         words = [sb.tile([P, 2 * M], U8, name="words%d" % i, align_bytes=64) for i in range(2)]
         planes = [sb.tile([P, M], U8, name="planes%d" % i, align_bytes=64) for i in range(2)]
         gate = sb.tile([P, G, N], F32, name="gate", align_bytes=64)
         y = sb.tile([P, G, N], F32, name="y", align_bytes=64)
-        y_raw = [sb.tile([P, PACK, HALF], F32, name="y_raw%d" % h, align_bytes=64) for h in range(2)]
+        y_bf = sb.tile([P, G, N], BF16, name="y_bf", align_bytes=64)
+        y_raw = [sb.tile([P, PACK, HALF], BF16, name="y_raw%d" % h, align_bytes=64) for h in range(2)]
         y_grp = [sb.tile([P, HALF, PACK], BF16, name="y_grp%d" % h, align_bytes=64) for h in range(2)]
         y_codes = [sb.tile([P, HALF], U32, name="y_codes%d" % h, align_bytes=64) for h in range(2)]
         y_scales = sb.tile([P, N], U8, name="y_scales", align_bytes=64)
         z = [[ps.tile([P, N], F32, name="z%d_%d" % (i, g)) for g in range(G)] for i in range(2)]
 
-        for i in range(2):
+        for i in (1, 0):
             nc.vector.memset(planes[i][:].bitcast(U32), 0)
+        nc.vector.memset(x_codes[:, 0:HALF], 0)
+        nc.vector.memset(x_scales[:, 0:HALF].bitcast(U32), 0)
 
         src_words = (w_words, u_words)
         src_scales = (w_scales, u_scales)
@@ -69,52 +73,69 @@ def tile_rows_pl_gswiglu4_kernel(tc, x, w_words, w_scales, u_words, u_scales, ou
                 out=words[h][:].bitcast(I32), in_=src_words[h].rearrange("g p b -> (g p) b").bitcast(I32)
             )
             nc.sync.dma_start(out=x_raw[h][:], in_=x_rows[:, :, halves[h]])
-        for i, queue in enumerate((nc.scalar, nc.sync)):
+        for i in range(2):
             for g in ORDER:
+                queue = nc.gpsimd if i == 1 and g != ORDER[-1] else nc.sync
                 queue.dma_start(
                     out=planes[i][ROWS * g : ROWS * g + 4, :].bitcast(I32), in_=src_scales[i][g].bitcast(I32)
                 )
 
-        for h in range(2):
-            interleave(nc.vector.tensor_copy, x_grp[h], x_raw[h], 0, HALF)
-            quantise(nc, x_codes[:, halves[h]], x_scales[:, halves[h]], x_grp[h])
-
-        for i in range(2):
-            for g in ORDER:
-                rows = slice(ROWS * g, ROWS * (g + 1))
-                nc.tensor.matmul_mx(
-                    out=z[i][g][:],
-                    lhsT=words[i][rows, :].bitcast(FP4X4),
-                    lhsT_scale=planes[i][rows, :],
-                    rhs=x_codes[rows, :].bitcast(FP8X4),
-                    rhs_scale=x_scales[rows, :],
-                    start=True,
-                    stop=True,
+        def quantise_x(h):
+            for q in range(2):
+                interleave(nc.vector.tensor_copy, x_grp[h], x_raw[h], q * QUARTER, (q + 1) * QUARTER)
+            for q in range(2):
+                c0 = HALF + h * HALF + q * QUARTER
+                nc.vector.quantize_mx(
+                    out=x_codes[:, c0 : c0 + QUARTER].bitcast(FP8X4),
+                    scales=x_scales[:, c0 : c0 + QUARTER],
+                    in_=x_grp[h][:, q * QUARTER : (q + 1) * QUARTER, :].rearrange("p n t -> p (n t)"),
                 )
 
-        chunks = [(h, g) for h in range(2) for g in ORDER]
-
-        def regroup(k):
-            h, g = chunks[k]
-            queue = nc.sync if g < 2 else nc.scalar
-            queue.dma_start(out=y_raw[h][ROWS * g : ROWS * (g + 1), :, :], in_=y[:, g, halves[h]])
-
-        LAG = 2
-        for k, (h, g) in enumerate(chunks):
-            nc.scalar.activation(out=gate[:, g, halves[h]], in_=z[0][g][:, halves[h]], func=ACT.Silu)
-            nc.vector.tensor_tensor(
-                out=y[:, g, halves[h]], in0=z[1][g][:, halves[h]], in1=gate[:, g, halves[h]], op=ALU.mult
+        def product(i, g, h):
+            rows = slice(ROWS * g, ROWS * (g + 1))
+            window = slice(h * HALF, h * HALF + N)
+            nc.tensor.matmul_mx(
+                out=z[i][g][:],
+                lhsT=words[i][rows, :].bitcast(FP4X4),
+                lhsT_scale=planes[i][rows, :],
+                rhs=x_codes[rows, window].bitcast(FP8X4),
+                rhs_scale=x_scales[rows, window],
+                start=True,
+                stop=True,
             )
-            if k >= LAG:
-                regroup(k - LAG)
-        for k in range(len(chunks) - LAG, len(chunks)):
-            regroup(k)
-        nc.scalar.dma_start(out=out_0.rearrange("(g m) n -> m g n", g=G), in_=y[:])
+
+        def silu(g, h):
+            nc.scalar.activation(out=gate[:, g, halves[h]], in_=z[0][g][:, halves[1]], func=ACT.Silu)
+
+        def gate_and_regroup(g, h):
+            nc.vector.tensor_tensor(
+                out=y_bf[:, g, halves[h]], in0=z[1][g][:, halves[1]], in1=gate[:, g, halves[h]], op=ALU.mult
+            )
+            nc.sync.dma_start(out=y_raw[h][ROWS * g : ROWS * (g + 1), :, :], in_=y_bf[:, g, halves[h]])
+
+        quantise_x(0)
+        for i in range(2):
+            for g in ORDER:
+                product(i, g, 0)
+        quantise_x(1)
+        for g in ORDER:
+            silu(g, 0)
+            gate_and_regroup(g, 0)
+        g0, g1, g2, g3 = ORDER
+        for i, g in ((0, g0), (0, g1), (0, g2), (1, g0), (0, g3), (1, g1), (1, g2), (1, g3)):
+            product(i, g, 1)
+        for g in ORDER:
+            silu(g, 1)
+            gate_and_regroup(g, 1)
+        for g in ORDER:
+            nc.vector.tensor_tensor(out=y[:, g, :], in0=z[1][g][:], in1=gate[:, g, :], op=ALU.mult)
+            nc.sync.dma_start(out=out_0[M * g : M * (g + 1), :], in_=y[:, g, :])
 
         out_words = out_1[0].rearrange("p n t -> p (n t)").bitcast(I32)
+        interleave(nc.scalar.copy, y_grp[0], y_raw[0], 0, HALF)
+        interleave(nc.vector.tensor_copy, y_grp[1], y_raw[1], 0, SPLIT)
+        interleave(nc.scalar.copy, y_grp[1], y_raw[1], SPLIT, HALF)
         for h in range(2):
-            interleave(nc.vector.tensor_copy, y_grp[h], y_raw[h], 0, SPLIT)
-            interleave(nc.scalar.copy, y_grp[h], y_raw[h], SPLIT, HALF)
             quantise(nc, y_codes[h][:], y_scales[:, halves[h]], y_grp[h])
             nc.sync.dma_start(out=out_words[:, halves[h]], in_=y_codes[h][:].bitcast(I32))
         for q in range(4):

@@ -20,7 +20,8 @@ PACK = 4
 ROWS = D // PACK
 HALF = N // 2
 ORDER = (0, 2, 1, 3)
-SPLIT = 192
+SPLIT = 128
+X_SPLIT = 160
 QUARTER = HALF // 2
 
 
@@ -59,6 +60,7 @@ def tile_rows_pl_gswiglu4_kernel(tc, x, w_words, w_scales, u_words, u_scales, ou
         y_grp = [sb.tile([P, HALF, PACK], BF16, name="y_grp%d" % h, align_bytes=64) for h in range(2)]
         y_codes = [sb.tile([P, HALF], U32, name="y_codes%d" % h, align_bytes=64) for h in range(2)]
         y_scales = sb.tile([P, N], U8, name="y_scales", align_bytes=64)
+        warm = sb.tile([P, 1], F32, name="warm", align_bytes=64)
         z = [[ps.tile([P, N], F32, name="z%d_%d" % (i, g)) for g in range(G)] for i in range(2)]
 
         for i in (1, 0):
@@ -68,21 +70,35 @@ def tile_rows_pl_gswiglu4_kernel(tc, x, w_words, w_scales, u_words, u_scales, ou
 
         src_words = (w_words, u_words)
         src_scales = (w_scales, u_scales)
-        for h in range(2):
-            nc.scalar.dma_start(
-                out=words[h][:].bitcast(I32), in_=src_words[h].rearrange("g p b -> (g p) b").bitcast(I32)
+
+        def load_words(queue, i):
+            queue.dma_start(
+                out=words[i][:].bitcast(I32), in_=src_words[i].rearrange("g p b -> (g p) b").bitcast(I32)
             )
+
+        def load_scales(queue, i, g):
+            queue.dma_start(
+                out=planes[i][ROWS * g : ROWS * g + 4, :].bitcast(I32), in_=src_scales[i][g].bitcast(I32)
+            )
+
+        def load_x(h):
             nc.sync.dma_start(out=x_raw[h][:], in_=x_rows[:, :, halves[h]])
-        for i in range(2):
-            for g in ORDER:
-                queue = nc.gpsimd if i == 1 and g != ORDER[-1] else nc.sync
-                queue.dma_start(
-                    out=planes[i][ROWS * g : ROWS * g + 4, :].bitcast(I32), in_=src_scales[i][g].bitcast(I32)
-                )
+
+        load_words(nc.scalar, 0)
+        load_x(0)
+        load_words(nc.scalar, 1)
+        for g in ORDER:
+            load_scales(nc.sync, 0, g)
+        load_x(1)
+        for g in ORDER:
+            load_scales(nc.sync if g == ORDER[-1] else nc.gpsimd, 1, g)
+
+        nc.scalar.activation(out=warm[:], in_=x_scales[:, 0:4].bitcast(F32), func=ACT.Silu)
 
         def quantise_x(h):
-            for q in range(2):
-                interleave(nc.vector.tensor_copy, x_grp[h], x_raw[h], q * QUARTER, (q + 1) * QUARTER)
+            interleave(nc.scalar.copy, x_grp[h], x_raw[h], X_SPLIT, HALF)
+            interleave(nc.vector.tensor_copy, x_grp[h], x_raw[h], 0, QUARTER)
+            interleave(nc.vector.tensor_copy, x_grp[h], x_raw[h], QUARTER, X_SPLIT)
             for q in range(2):
                 c0 = HALF + h * HALF + q * QUARTER
                 nc.vector.quantize_mx(
@@ -124,20 +140,27 @@ def tile_rows_pl_gswiglu4_kernel(tc, x, w_words, w_scales, u_words, u_scales, ou
         g0, g1, g2, g3 = ORDER
         for i, g in ((0, g0), (0, g1), (0, g2), (1, g0), (0, g3), (1, g1), (1, g2), (1, g3)):
             product(i, g, 1)
+        def gate_f32(g, cols):
+            nc.vector.tensor_tensor(out=y[:, g, cols], in0=z[1][g][:, cols], in1=gate[:, g, cols], op=ALU.mult)
+
+        def store(g):
+            nc.sync.dma_start(out=out_0[M * g : M * (g + 1), :], in_=y[:, g, :])
+
         for g in ORDER:
             silu(g, 1)
             gate_and_regroup(g, 1)
         for g in ORDER:
-            nc.vector.tensor_tensor(out=y[:, g, :], in0=z[1][g][:], in1=gate[:, g, :], op=ALU.mult)
-            nc.sync.dma_start(out=out_0[M * g : M * (g + 1), :], in_=y[:, g, :])
+            gate_f32(g, slice(0, N))
+            store(g)
 
         out_words = out_1[0].rearrange("p n t -> p (n t)").bitcast(I32)
         interleave(nc.scalar.copy, y_grp[0], y_raw[0], 0, HALF)
-        interleave(nc.vector.tensor_copy, y_grp[1], y_raw[1], 0, SPLIT)
         interleave(nc.scalar.copy, y_grp[1], y_raw[1], SPLIT, HALF)
-        for h in range(2):
-            quantise(nc, y_codes[h][:], y_scales[:, halves[h]], y_grp[h])
-            nc.sync.dma_start(out=out_words[:, halves[h]], in_=y_codes[h][:].bitcast(I32))
+        quantise(nc, y_codes[0][:], y_scales[:, halves[0]], y_grp[0])
+        nc.sync.dma_start(out=out_words[:, halves[0]], in_=y_codes[0][:].bitcast(I32))
+        interleave(nc.vector.tensor_copy, y_grp[1], y_raw[1], 0, SPLIT)
+        quantise(nc, y_codes[1][:], y_scales[:, halves[1]], y_grp[1])
+        nc.sync.dma_start(out=out_words[:, halves[1]], in_=y_codes[1][:].bitcast(I32))
         for q in range(4):
             queue = nc.scalar if q < 2 else nc.sync
             queue.dma_start(

@@ -20,7 +20,7 @@ PACK = 4
 ROWS = D // PACK
 HALF = N // 2
 ORDER = (0, 2, 1, 3)
-SPLIT = 128
+SPLIT = 192
 X_SPLIT = 160
 QUARTER = HALF // 2
 
@@ -63,7 +63,7 @@ def tile_rows_pl_gswiglu4_kernel(tc, x, w_words, w_scales, u_words, u_scales, ou
         warm = sb.tile([P, 1], F32, name="warm", align_bytes=64)
         z = [[ps.tile([P, N], F32, name="z%d_%d" % (i, g)) for g in range(G)] for i in range(2)]
 
-        for i in (1, 0):
+        for i in range(2):
             nc.vector.memset(planes[i][:].bitcast(U32), 0)
         nc.vector.memset(x_codes[:, 0:HALF], 0)
         nc.vector.memset(x_scales[:, 0:HALF].bitcast(U32), 0)
@@ -84,14 +84,16 @@ def tile_rows_pl_gswiglu4_kernel(tc, x, w_words, w_scales, u_words, u_scales, ou
         def load_x(h):
             nc.sync.dma_start(out=x_raw[h][:], in_=x_rows[:, :, halves[h]])
 
+        g0, g1, g2, g3 = ORDER
         load_words(nc.scalar, 0)
         load_x(0)
         load_words(nc.scalar, 1)
-        for g in ORDER:
-            load_scales(nc.sync, 0, g)
+        for i, g in ((0, g0), (1, g0), (0, g1), (1, g1)):
+            load_scales(nc.sync, i, g)
         load_x(1)
-        for g in ORDER:
-            load_scales(nc.sync if g == ORDER[-1] else nc.gpsimd, 1, g)
+        load_scales(nc.sync, 0, g2)
+        for i, g in ((0, g3), (1, g2), (1, g3)):
+            load_scales(nc.gpsimd, i, g)
 
         nc.scalar.activation(out=warm[:], in_=x_scales[:, 0:4].bitcast(F32), func=ACT.Silu)
 
@@ -130,14 +132,12 @@ def tile_rows_pl_gswiglu4_kernel(tc, x, w_words, w_scales, u_words, u_scales, ou
             nc.sync.dma_start(out=y_raw[h][ROWS * g : ROWS * (g + 1), :, :], in_=y_bf[:, g, halves[h]])
 
         quantise_x(0)
-        for i in range(2):
-            for g in ORDER:
-                product(i, g, 0)
+        for i, g in ((0, g0), (0, g1), (1, g0), (1, g1), (0, g2), (0, g3), (1, g2), (1, g3)):
+            product(i, g, 0)
         quantise_x(1)
         for g in ORDER:
             silu(g, 0)
             gate_and_regroup(g, 0)
-        g0, g1, g2, g3 = ORDER
         for i, g in ((0, g0), (0, g1), (0, g2), (1, g0), (0, g3), (1, g1), (1, g2), (1, g3)):
             product(i, g, 1)
         def gate_f32(g, cols):
@@ -156,9 +156,9 @@ def tile_rows_pl_gswiglu4_kernel(tc, x, w_words, w_scales, u_words, u_scales, ou
         out_words = out_1[0].rearrange("p n t -> p (n t)").bitcast(I32)
         interleave(nc.scalar.copy, y_grp[0], y_raw[0], 0, HALF)
         interleave(nc.scalar.copy, y_grp[1], y_raw[1], SPLIT, HALF)
+        interleave(nc.vector.tensor_copy, y_grp[1], y_raw[1], 0, SPLIT)
         quantise(nc, y_codes[0][:], y_scales[:, halves[0]], y_grp[0])
         nc.sync.dma_start(out=out_words[:, halves[0]], in_=y_codes[0][:].bitcast(I32))
-        interleave(nc.vector.tensor_copy, y_grp[1], y_raw[1], 0, SPLIT)
         quantise(nc, y_codes[1][:], y_scales[:, halves[1]], y_grp[1])
         nc.sync.dma_start(out=out_words[:, halves[1]], in_=y_codes[1][:].bitcast(I32))
         for q in range(4):

@@ -85,15 +85,15 @@ def tile_rows_pl_gswiglu4_kernel(tc, x, w_words, w_scales, u_words, u_scales, ou
             nc.sync.dma_start(out=x_raw[h][:], in_=x_rows[:, :, halves[h]])
 
         g0, g1, g2, g3 = ORDER
-        load_words(nc.scalar, 0)
         load_x(0)
-        load_words(nc.scalar, 1)
-        for i, g in ((0, g0), (1, g0), (0, g1), (1, g1)):
-            load_scales(nc.sync, i, g)
+        for i in range(2):
+            load_words(nc.sync, i)
+            for g in (g0, g1):
+                load_scales(nc.sync, i, g)
         load_x(1)
-        load_scales(nc.sync, 0, g2)
-        for i, g in ((0, g3), (1, g2), (1, g3)):
-            load_scales(nc.gpsimd, i, g)
+        for i in range(2):
+            for g in (g2, g3):
+                load_scales(nc.sync, i, g)
 
         nc.scalar.activation(out=warm[:], in_=x_scales[:, 0:4].bitcast(F32), func=ACT.Silu)
 

@@ -85,14 +85,10 @@ def tile_rows_pl_gswiglu4_kernel(tc, x, w_words, w_scales, u_words, u_scales, ou
             nc.sync.dma_start(out=x_raw[h][:], in_=x_rows[:, :, halves[h]])
 
         g0, g1, g2, g3 = ORDER
-        load_x(0)
         for i in range(2):
+            load_x(i)
             load_words(nc.sync, i)
-            for g in (g0, g1):
-                load_scales(nc.sync, i, g)
-        load_x(1)
-        for i in range(2):
-            for g in (g2, g3):
+            for g in ORDER:
                 load_scales(nc.sync, i, g)
 
         nc.scalar.activation(out=warm[:], in_=x_scales[:, 0:4].bitcast(F32), func=ACT.Silu)
@@ -132,8 +128,9 @@ def tile_rows_pl_gswiglu4_kernel(tc, x, w_words, w_scales, u_words, u_scales, ou
             nc.sync.dma_start(out=y_raw[h][ROWS * g : ROWS * (g + 1), :, :], in_=y_bf[:, g, halves[h]])
 
         quantise_x(0)
-        for i, g in ((0, g0), (0, g1), (1, g0), (1, g1), (0, g2), (0, g3), (1, g2), (1, g3)):
-            product(i, g, 0)
+        for i in range(2):
+            for g in ORDER:
+                product(i, g, 0)
         quantise_x(1)
         for g in ORDER:
             silu(g, 0)

@@ -20,7 +20,7 @@ PACK = 4
 ROWS = D // PACK
 HALF = N // 2
 ORDER = (0, 2, 1, 3)
-SPLIT = 192
+SPLIT = 160
 X_SPLIT = 160
 QUARTER = HALF // 2
 

@@ -159,7 +159,7 @@ def tile_rows_pl_gswiglu4_kernel(tc, x, w_words, w_scales, u_words, u_scales, ou
         quantise(nc, y_codes[1][:], y_scales[:, halves[1]], y_grp[1])
         nc.sync.dma_start(out=out_words[:, halves[1]], in_=y_codes[1][:].bitcast(I32))
         for q in range(4):
-            queue = nc.scalar if q < 2 else nc.sync
+            queue = nc.scalar if q < 3 else nc.sync
             queue.dma_start(
                 out=out_2[0, 4 * q : 4 * q + 4, :].bitcast(I32),
                 in_=y_scales[32 * q : 32 * q + 4, :].bitcast(I32),

@@ -19,22 +19,17 @@ P = 128
 PACK = 4
 ROWS = D // PACK
 HALF = N // 2
-ORDER = (0, 2, 1, 3)
-SPLIT = 160
-X_SPLIT = 160
 QUARTER = HALF // 2
+ORDER = (0, 2, 1, 3)
+X_SPLIT = 160
+Y_SPLIT = 160
+POOL_FIRST = 192
 
 
 def interleave(copy, dst, src, c0, c1):
     copy(
         out=dst[:, c0:c1, :].rearrange("p (c i) t -> p c t i", i=4),
         in_=src[:, :, c0:c1].rearrange("p t (c i) -> p c t i", i=4),
-    )
-
-
-def quantise(nc, codes, scales, grouped):
-    nc.vector.quantize_mx(
-        out=codes.bitcast(FP8X4), scales=scales, in_=grouped[:].rearrange("p n t -> p (n t)")
     )
 
 
@@ -61,6 +56,7 @@ def tile_rows_pl_gswiglu4_kernel(tc, x, w_words, w_scales, u_words, u_scales, ou
         y_codes = [sb.tile([P, HALF], U32, name="y_codes%d" % h, align_bytes=64) for h in range(2)]
         y_scales = sb.tile([P, N], U8, name="y_scales", align_bytes=64)
         warm = sb.tile([P, 1], F32, name="warm", align_bytes=64)
+        u_sb = [sb.tile([P, HALF], F32, name="u_sb%d" % k, align_bytes=64) for k in range(2)]
         z = [[ps.tile([P, N], F32, name="z%d_%d" % (i, g)) for g in range(G)] for i in range(2)]
 
         for i in range(2):
@@ -70,40 +66,34 @@ def tile_rows_pl_gswiglu4_kernel(tc, x, w_words, w_scales, u_words, u_scales, ou
 
         src_words = (w_words, u_words)
         src_scales = (w_scales, u_scales)
+        out_words = out_1[0].rearrange("p n t -> p (n t)").bitcast(I32)
+        g0, g1, g2, g3 = ORDER
 
-        def load_words(queue, i):
-            queue.dma_start(
+        def load_words(i):
+            nc.sync.dma_start(
                 out=words[i][:].bitcast(I32), in_=src_words[i].rearrange("g p b -> (g p) b").bitcast(I32)
             )
 
-        def load_scales(queue, i, g):
-            queue.dma_start(
+        def load_scales(i, g):
+            nc.sync.dma_start(
                 out=planes[i][ROWS * g : ROWS * g + 4, :].bitcast(I32), in_=src_scales[i][g].bitcast(I32)
             )
 
         def load_x(h):
             nc.sync.dma_start(out=x_raw[h][:], in_=x_rows[:, :, halves[h]])
 
-        g0, g1, g2, g3 = ORDER
-        for i in range(2):
-            load_x(i)
-            load_words(nc.sync, i)
-            for g in ORDER:
-                load_scales(nc.sync, i, g)
-
-        nc.scalar.activation(out=warm[:], in_=x_scales[:, 0:4].bitcast(F32), func=ACT.Silu)
-
-        def quantise_x(h):
+        def interleave_x(h):
             interleave(nc.scalar.copy, x_grp[h], x_raw[h], X_SPLIT, HALF)
             interleave(nc.vector.tensor_copy, x_grp[h], x_raw[h], 0, QUARTER)
             interleave(nc.vector.tensor_copy, x_grp[h], x_raw[h], QUARTER, X_SPLIT)
-            for q in range(2):
-                c0 = HALF + h * HALF + q * QUARTER
-                nc.vector.quantize_mx(
-                    out=x_codes[:, c0 : c0 + QUARTER].bitcast(FP8X4),
-                    scales=x_scales[:, c0 : c0 + QUARTER],
-                    in_=x_grp[h][:, q * QUARTER : (q + 1) * QUARTER, :].rearrange("p n t -> p (n t)"),
-                )
+
+        def quantise_x(h, q):
+            c0 = HALF + h * HALF + q * QUARTER
+            nc.vector.quantize_mx(
+                out=x_codes[:, c0 : c0 + QUARTER].bitcast(FP8X4),
+                scales=x_scales[:, c0 : c0 + QUARTER],
+                in_=x_grp[h][:, q * QUARTER : (q + 1) * QUARTER, :].rearrange("p n t -> p (n t)"),
+            )
 
         def product(i, g, h):
             rows = slice(ROWS * g, ROWS * (g + 1))
@@ -121,46 +111,79 @@ def tile_rows_pl_gswiglu4_kernel(tc, x, w_words, w_scales, u_words, u_scales, ou
         def silu(g, h):
             nc.scalar.activation(out=gate[:, g, halves[h]], in_=z[0][g][:, halves[1]], func=ACT.Silu)
 
-        def gate_and_regroup(g, h):
+        def gate_bf16(g, h):
             nc.vector.tensor_tensor(
                 out=y_bf[:, g, halves[h]], in0=z[1][g][:, halves[1]], in1=gate[:, g, halves[h]], op=ALU.mult
             )
-            nc.sync.dma_start(out=y_raw[h][ROWS * g : ROWS * (g + 1), :, :], in_=y_bf[:, g, halves[h]])
 
-        quantise_x(0)
-        for i in range(2):
-            for g in ORDER:
-                product(i, g, 0)
-        quantise_x(1)
-        for g in ORDER:
-            silu(g, 0)
-            gate_and_regroup(g, 0)
-        for i, g in ((0, g0), (0, g1), (0, g2), (1, g0), (0, g3), (1, g1), (1, g2), (1, g3)):
-            product(i, g, 1)
         def gate_f32(g, cols):
             nc.vector.tensor_tensor(out=y[:, g, cols], in0=z[1][g][:, cols], in1=gate[:, g, cols], op=ALU.mult)
 
-        def store(g):
-            nc.sync.dma_start(out=out_0[M * g : M * (g + 1), :], in_=y[:, g, :])
+        def regroup(g, h):
+            nc.sync.dma_start(out=y_raw[h][ROWS * g : ROWS * (g + 1), :, :], in_=y_bf[:, g, halves[h]])
 
+        def store(g, cols):
+            nc.sync.dma_start(out=out_0[M * g : M * (g + 1), cols], in_=y[:, g, cols])
+
+        def quantise_y(h, c0, c1):
+            nc.vector.quantize_mx(
+                out=y_codes[h][:, c0:c1].bitcast(FP8X4),
+                scales=y_scales[:, h * HALF + c0 : h * HALF + c1],
+                in_=y_grp[h][:, c0:c1, :].rearrange("p n t -> p (n t)"),
+            )
+
+        def store_words(h):
+            nc.sync.dma_start(out=out_words[:, halves[h]], in_=y_codes[h][:].bitcast(I32))
+
+        def store_scales():
+            for q in range(4):
+                queue = nc.scalar if q < 3 else nc.sync
+                queue.dma_start(
+                    out=out_2[0, 4 * q : 4 * q + 4, :].bitcast(I32),
+                    in_=y_scales[32 * q : 32 * q + 4, :].bitcast(I32),
+                )
+
+        def gate_on_pool(k, g, cols):
+            nc.scalar.copy(out=u_sb[k][:, cols], in_=z[1][g][:, cols])
+            nc.gpsimd.tensor_tensor(out=y[:, g, cols], in0=u_sb[k][:, cols], in1=gate[:, g, cols], op=ALU.mult)
+
+        for i in range(2):
+            load_x(i)
+            load_words(i)
+            for g in ORDER:
+                load_scales(i, g)
+
+        nc.scalar.activation(out=warm[:], in_=x_scales[:, 0:4].bitcast(F32), func=ACT.Silu)
+
+        interleave_x(0)
+        for q in range(2):
+            quantise_x(0, q)
+        for i in range(2):
+            for g in ORDER:
+                product(i, g, 0)
+        interleave_x(1)
+        for q in range(2):
+            quantise_x(1, q)
+        for g in ORDER:
+            silu(g, 0)
+            gate_bf16(g, 0)
+            regroup(g, 0)
+        for i, g in ((0, g0), (0, g1), (0, g2), (1, g0), (0, g3), (1, g1), (1, g2), (1, g3)):
+            product(i, g, 1)
         for g in ORDER:
             silu(g, 1)
-            gate_and_regroup(g, 1)
-        for g in ORDER:
-            gate_f32(g, slice(0, N))
-            store(g)
+            gate_bf16(g, 1)
+            regroup(g, 1)
+        gate_on_pool(0, g0, slice(0, POOL_FIRST))
+        gate_on_pool(1, g3, halves[0])
+        for g, c0 in ((g0, POOL_FIRST), (g1, 0), (g2, 0), (g3, HALF)):
+            gate_f32(g, slice(c0, N))
+            store(g, slice(0, N))
 
-        out_words = out_1[0].rearrange("p n t -> p (n t)").bitcast(I32)
         interleave(nc.scalar.copy, y_grp[0], y_raw[0], 0, HALF)
-        interleave(nc.scalar.copy, y_grp[1], y_raw[1], SPLIT, HALF)
-        interleave(nc.vector.tensor_copy, y_grp[1], y_raw[1], 0, SPLIT)
-        quantise(nc, y_codes[0][:], y_scales[:, halves[0]], y_grp[0])
-        nc.sync.dma_start(out=out_words[:, halves[0]], in_=y_codes[0][:].bitcast(I32))
-        quantise(nc, y_codes[1][:], y_scales[:, halves[1]], y_grp[1])
-        nc.sync.dma_start(out=out_words[:, halves[1]], in_=y_codes[1][:].bitcast(I32))
-        for q in range(4):
-            queue = nc.scalar if q < 3 else nc.sync
-            queue.dma_start(
-                out=out_2[0, 4 * q : 4 * q + 4, :].bitcast(I32),
-                in_=y_scales[32 * q : 32 * q + 4, :].bitcast(I32),
-            )
+        interleave(nc.scalar.copy, y_grp[1], y_raw[1], Y_SPLIT, HALF)
+        interleave(nc.vector.tensor_copy, y_grp[1], y_raw[1], 0, Y_SPLIT)
+        for h in range(2):
+            quantise_y(h, 0, HALF)
+            store_words(h)
+        store_scales()

@@ -23,7 +23,7 @@ QUARTER = HALF // 2
 ORDER = (0, 2, 1, 3)
 X_SPLIT = 160
 Y_SPLIT = 160
-POOL_FIRST = 192
+POOL_FIRST = 128
 
 
 def interleave(copy, dst, src, c0, c1):

@@ -22,7 +22,6 @@ HALF = N // 2
 QUARTER = HALF // 2
 ORDER = (0, 2, 1, 3)
 X_SPLIT = 160
-Y_SPLIT = 160
 POOL_FIRST = 128
 
 
@@ -52,11 +51,11 @@ def tile_rows_pl_gswiglu4_kernel(tc, x, w_words, w_scales, u_words, u_scales, ou
         y = sb.tile([P, G, N], F32, name="y", align_bytes=64)
         y_bf = sb.tile([P, G, N], BF16, name="y_bf", align_bytes=64)
         y_raw = [sb.tile([P, PACK, HALF], BF16, name="y_raw%d" % h, align_bytes=64) for h in range(2)]
-        y_grp = [sb.tile([P, HALF, PACK], BF16, name="y_grp%d" % h, align_bytes=64) for h in range(2)]
-        y_codes = [sb.tile([P, HALF], U32, name="y_codes%d" % h, align_bytes=64) for h in range(2)]
+        y_grp = sb.tile([P, N, PACK], BF16, name="y_grp", align_bytes=64)
+        y_codes = sb.tile([P, N], U32, name="y_codes", align_bytes=64)
         y_scales = sb.tile([P, N], U8, name="y_scales", align_bytes=64)
         warm = sb.tile([P, 1], F32, name="warm", align_bytes=64)
-        u_sb = [sb.tile([P, HALF], F32, name="u_sb%d" % k, align_bytes=64) for k in range(2)]
+        u_sb = sb.tile([P, G, N], F32, name="u_sb", align_bytes=64)
         z = [[ps.tile([P, N], F32, name="z%d_%d" % (i, g)) for g in range(G)] for i in range(2)]
 
         for i in range(2):
@@ -108,32 +107,39 @@ def tile_rows_pl_gswiglu4_kernel(tc, x, w_words, w_scales, u_words, u_scales, ou
                 stop=True,
             )
 
-        def silu(g, h):
-            nc.scalar.activation(out=gate[:, g, halves[h]], in_=z[0][g][:, halves[1]], func=ACT.Silu)
+        def silu(g, c0, c1, shift=0):
+            nc.scalar.activation(out=gate[:, g, c0:c1], in_=z[0][g][:, c0 + shift : c1 + shift], func=ACT.Silu)
 
-        def gate_bf16(g, h):
+        def gate_bf16(g, c0, c1, shift=0):
             nc.vector.tensor_tensor(
-                out=y_bf[:, g, halves[h]], in0=z[1][g][:, halves[1]], in1=gate[:, g, halves[h]], op=ALU.mult
+                out=y_bf[:, g, c0:c1], in0=z[1][g][:, c0 + shift : c1 + shift], in1=gate[:, g, c0:c1], op=ALU.mult
             )
 
-        def gate_f32(g, cols):
-            nc.vector.tensor_tensor(out=y[:, g, cols], in0=z[1][g][:, cols], in1=gate[:, g, cols], op=ALU.mult)
+        def gate_f32(g, c0, c1):
+            nc.vector.tensor_tensor(out=y[:, g, c0:c1], in0=z[1][g][:, c0:c1], in1=gate[:, g, c0:c1], op=ALU.mult)
 
-        def regroup(g, h):
-            nc.sync.dma_start(out=y_raw[h][ROWS * g : ROWS * (g + 1), :, :], in_=y_bf[:, g, halves[h]])
+        def regroup(g, c0, c1, queue=nc.sync):
+            h = c0 // HALF
+            queue.dma_start(
+                out=y_raw[h][ROWS * g : ROWS * (g + 1), :, c0 - h * HALF : c1 - h * HALF], in_=y_bf[:, g, c0:c1]
+            )
 
-        def store(g, cols):
-            nc.sync.dma_start(out=out_0[M * g : M * (g + 1), cols], in_=y[:, g, cols])
+        def store(g):
+            nc.sync.dma_start(out=out_0[M * g : M * (g + 1), :], in_=y[:, g, :])
 
-        def quantise_y(h, c0, c1):
+        def interleave_y(copy, c0, c1):
+            h = c0 // HALF
+            interleave(copy, y_grp[:, halves[h], :], y_raw[h], c0 - h * HALF, c1 - h * HALF)
+
+        def quantise_y(c0, c1):
             nc.vector.quantize_mx(
-                out=y_codes[h][:, c0:c1].bitcast(FP8X4),
-                scales=y_scales[:, h * HALF + c0 : h * HALF + c1],
-                in_=y_grp[h][:, c0:c1, :].rearrange("p n t -> p (n t)"),
+                out=y_codes[:, c0:c1].bitcast(FP8X4),
+                scales=y_scales[:, c0:c1],
+                in_=y_grp[:, c0:c1, :].rearrange("p n t -> p (n t)"),
             )
 
-        def store_words(h):
-            nc.sync.dma_start(out=out_words[:, halves[h]], in_=y_codes[h][:].bitcast(I32))
+        def store_words(c0, c1, queue=nc.sync):
+            queue.dma_start(out=out_words[:, c0:c1], in_=y_codes[:, c0:c1].bitcast(I32))
 
         def store_scales():
             for q in range(4):
@@ -143,9 +149,9 @@ def tile_rows_pl_gswiglu4_kernel(tc, x, w_words, w_scales, u_words, u_scales, ou
                     in_=y_scales[32 * q : 32 * q + 4, :].bitcast(I32),
                 )
 
-        def gate_on_pool(k, g, cols):
-            nc.scalar.copy(out=u_sb[k][:, cols], in_=z[1][g][:, cols])
-            nc.gpsimd.tensor_tensor(out=y[:, g, cols], in0=u_sb[k][:, cols], in1=gate[:, g, cols], op=ALU.mult)
+        def gate_on_pool(g, c0, c1):
+            nc.scalar.copy(out=u_sb[:, g, c0:c1], in_=z[1][g][:, c0:c1])
+            nc.gpsimd.tensor_tensor(out=y[:, g, c0:c1], in0=u_sb[:, g, c0:c1], in1=gate[:, g, c0:c1], op=ALU.mult)
 
         for i in range(2):
             load_x(i)
@@ -165,25 +171,29 @@ def tile_rows_pl_gswiglu4_kernel(tc, x, w_words, w_scales, u_words, u_scales, ou
         for q in range(2):
             quantise_x(1, q)
         for g in ORDER:
-            silu(g, 0)
-            gate_bf16(g, 0)
-            regroup(g, 0)
+            silu(g, 0, HALF, HALF)
+            gate_bf16(g, 0, HALF, HALF)
+            regroup(g, 0, HALF)
         for i, g in ((0, g0), (0, g1), (0, g2), (1, g0), (0, g3), (1, g1), (1, g2), (1, g3)):
             product(i, g, 1)
-        for g in ORDER:
-            silu(g, 1)
-            gate_bf16(g, 1)
-            regroup(g, 1)
-        gate_on_pool(0, g0, slice(0, POOL_FIRST))
-        gate_on_pool(1, g3, halves[0])
+        third = HALF + QUARTER
+        pieces = [(g0, HALF, N), (g1, HALF, N), (g2, HALF, third), (g3, HALF, third), (g2, third, N), (g3, third, N)]
+        for g, c0, c1 in pieces:
+            silu(g, c0, c1)
+            gate_bf16(g, c0, c1)
+            regroup(g, c0, c1)
+        gate_on_pool(g0, 0, POOL_FIRST)
+        gate_on_pool(g3, 0, HALF)
         for g, c0 in ((g0, POOL_FIRST), (g1, 0), (g2, 0), (g3, HALF)):
-            gate_f32(g, slice(c0, N))
-            store(g, slice(0, N))
+            gate_f32(g, c0, N)
+            store(g)
 
-        interleave(nc.scalar.copy, y_grp[0], y_raw[0], 0, HALF)
-        interleave(nc.scalar.copy, y_grp[1], y_raw[1], Y_SPLIT, HALF)
-        interleave(nc.vector.tensor_copy, y_grp[1], y_raw[1], 0, Y_SPLIT)
-        for h in range(2):
-            quantise_y(h, 0, HALF)
-            store_words(h)
+        interleave_y(nc.scalar.copy, 0, HALF)
+        interleave_y(nc.scalar.copy, HALF, third)
+        quantise_y(0, HALF)
+        interleave_y(nc.vector.tensor_copy, third, N)
+        quantise_y(HALF, third)
+        store_words(0, third)
+        quantise_y(third, N)
+        store_words(third, N)
         store_scales()

@@ -22,7 +22,7 @@ HALF = N // 2
 QUARTER = HALF // 2
 ORDER = (0, 2, 1, 3)
 X_SPLIT = 160
-POOL_FIRST = 128
+Y_SPLIT = 352
 
 
 def interleave(copy, dst, src, c0, c1):
@@ -182,18 +182,20 @@ def tile_rows_pl_gswiglu4_kernel(tc, x, w_words, w_scales, u_words, u_scales, ou
             silu(g, c0, c1)
             gate_bf16(g, c0, c1)
             regroup(g, c0, c1)
-        gate_on_pool(g0, 0, POOL_FIRST)
+        gate_on_pool(g0, 0, QUARTER)
+        gate_on_pool(g2, 0, QUARTER)
         gate_on_pool(g3, 0, HALF)
-        for g, c0 in ((g0, POOL_FIRST), (g1, 0), (g2, 0), (g3, HALF)):
+        for g, c0 in ((g0, QUARTER), (g1, 0), (g2, QUARTER), (g3, HALF)):
             gate_f32(g, c0, N)
             store(g)
 
         interleave_y(nc.scalar.copy, 0, HALF)
-        interleave_y(nc.scalar.copy, HALF, third)
-        quantise_y(0, HALF)
+        interleave_y(nc.scalar.copy, HALF, Y_SPLIT)
+        interleave_y(nc.vector.tensor_copy, Y_SPLIT, third)
         interleave_y(nc.vector.tensor_copy, third, N)
+        quantise_y(0, HALF)
+        store_words(0, HALF)
         quantise_y(HALF, third)
-        store_words(0, third)
         quantise_y(third, N)
-        store_words(third, N)
+        store_words(HALF, N)
         store_scales()

from contextlib import ExitStack

import concourse.mybir as mybir

G, D, M, N = 4, 128, 128, 512
FLOPS = 2 * 2 * G * D * M * N

F32 = mybir.dt.float32
BF16 = mybir.dt.bfloat16
I32 = mybir.dt.int32
U32 = mybir.dt.uint32
U8 = mybir.dt.uint8
FP8X4 = mybir.dt.float8_e4m3fn_x4
FP4X4 = mybir.dt.float4_e2m1fn_x4
ACT = mybir.ActivationFunctionType
ALU = mybir.AluOpType

P = 128
PACK = 4
ROWS = D // PACK
HALF = N // 2
QUARTER = HALF // 2
ORDER = (0, 2, 1, 3)
X_SPLIT = 160
Y_SPLIT = 352


def interleave(copy, dst, src, c0, c1):
    copy(
        out=dst[:, c0:c1, :].rearrange("p (c i) t -> p c t i", i=4),
        in_=src[:, :, c0:c1].rearrange("p t (c i) -> p c t i", i=4),
    )


def tile_rows_pl_gswiglu4_kernel(tc, x, w_words, w_scales, u_words, u_scales, out_0, out_1, out_2):
    nc = tc.nc
    with ExitStack() as ctx:
        sb = ctx.enter_context(tc.tile_pool(name="sb", bufs=1))
        ps = ctx.enter_context(tc.psum_pool(name="ps", bufs=1))
        ctx.enter_context(tc.manual_schedule())

        halves = [slice(h * HALF, (h + 1) * HALF) for h in range(2)]
        x_rows = x.rearrange("g (p j) n -> (g p) j n", j=PACK)
        x_raw = [sb.tile([P, PACK, HALF], F32, name="x_raw%d" % h, align_bytes=64) for h in range(2)]
        x_grp = [sb.tile([P, HALF, PACK], BF16, name="x_grp%d" % h, align_bytes=64) for h in range(2)]
        x_codes = sb.tile([P, HALF + N], U32, name="x_codes", align_bytes=64)
        x_scales = sb.tile([P, HALF + N], U8, name="x_scales", align_bytes=64)
        words = [sb.tile([P, 2 * M], U8, name="words%d" % i, align_bytes=64) for i in range(2)]
        planes = [sb.tile([P, M], U8, name="planes%d" % i, align_bytes=64) for i in range(2)]
        gate = sb.tile([P, G, N], F32, name="gate", align_bytes=64)
        y = sb.tile([P, G, N], F32, name="y", align_bytes=64)
        y_bf = sb.tile([P, G, N], BF16, name="y_bf", align_bytes=64)
        y_raw = [sb.tile([P, PACK, HALF], BF16, name="y_raw%d" % h, align_bytes=64) for h in range(2)]
        y_grp = sb.tile([P, N, PACK], BF16, name="y_grp", align_bytes=64)
        y_codes = sb.tile([P, N], U32, name="y_codes", align_bytes=64)
        y_scales = sb.tile([P, N], U8, name="y_scales", align_bytes=64)
        warm = sb.tile([P, 1], F32, name="warm", align_bytes=64)
        u_sb = sb.tile([P, G, N], F32, name="u_sb", align_bytes=64)
        z = [[ps.tile([P, N], F32, name="z%d_%d" % (i, g)) for g in range(G)] for i in range(2)]

        for i in range(2):
            nc.vector.memset(planes[i][:].bitcast(U32), 0)
        nc.vector.memset(x_codes[:, 0:HALF], 0)
        nc.vector.memset(x_scales[:, 0:HALF].bitcast(U32), 0)

        src_words = (w_words, u_words)
        src_scales = (w_scales, u_scales)
        out_words = out_1[0].rearrange("p n t -> p (n t)").bitcast(I32)
        g0, g1, g2, g3 = ORDER

        def load_words(i):
            nc.sync.dma_start(
                out=words[i][:].bitcast(I32), in_=src_words[i].rearrange("g p b -> (g p) b").bitcast(I32)
            )

        def load_scales(i, g):
            nc.sync.dma_start(
                out=planes[i][ROWS * g : ROWS * g + 4, :].bitcast(I32), in_=src_scales[i][g].bitcast(I32)
            )

        def load_x(h):
            nc.sync.dma_start(out=x_raw[h][:], in_=x_rows[:, :, halves[h]])

        def interleave_x(h):
            interleave(nc.scalar.copy, x_grp[h], x_raw[h], X_SPLIT, HALF)
            interleave(nc.vector.tensor_copy, x_grp[h], x_raw[h], 0, QUARTER)
            interleave(nc.vector.tensor_copy, x_grp[h], x_raw[h], QUARTER, X_SPLIT)

        def quantise_x(h, q):
            c0 = HALF + h * HALF + q * QUARTER
            nc.vector.quantize_mx(
                out=x_codes[:, c0 : c0 + QUARTER].bitcast(FP8X4),
                scales=x_scales[:, c0 : c0 + QUARTER],
                in_=x_grp[h][:, q * QUARTER : (q + 1) * QUARTER, :].rearrange("p n t -> p (n t)"),
            )

        def product(i, g, h):
            rows = slice(ROWS * g, ROWS * (g + 1))
            window = slice(h * HALF, h * HALF + N)
            nc.tensor.matmul_mx(
                out=z[i][g][:],
                lhsT=words[i][rows, :].bitcast(FP4X4),
                lhsT_scale=planes[i][rows, :],
                rhs=x_codes[rows, window].bitcast(FP8X4),
                rhs_scale=x_scales[rows, window],
                start=True,
                stop=True,
            )

        def silu(g, c0, c1, shift=0):
            nc.scalar.activation(out=gate[:, g, c0:c1], in_=z[0][g][:, c0 + shift : c1 + shift], func=ACT.Silu)

        def gate_bf16(g, c0, c1, shift=0):
            nc.vector.tensor_tensor(
                out=y_bf[:, g, c0:c1], in0=z[1][g][:, c0 + shift : c1 + shift], in1=gate[:, g, c0:c1], op=ALU.mult
            )

        def gate_f32(g, c0, c1):
            nc.vector.tensor_tensor(out=y[:, g, c0:c1], in0=z[1][g][:, c0:c1], in1=gate[:, g, c0:c1], op=ALU.mult)

        def regroup(g, c0, c1, queue=nc.sync):
            h = c0 // HALF
            queue.dma_start(
                out=y_raw[h][ROWS * g : ROWS * (g + 1), :, c0 - h * HALF : c1 - h * HALF], in_=y_bf[:, g, c0:c1]
            )

        def store(g):
            nc.sync.dma_start(out=out_0[M * g : M * (g + 1), :], in_=y[:, g, :])

        def interleave_y(copy, c0, c1):
            h = c0 // HALF
            interleave(copy, y_grp[:, halves[h], :], y_raw[h], c0 - h * HALF, c1 - h * HALF)

        def quantise_y(c0, c1):
            nc.vector.quantize_mx(
                out=y_codes[:, c0:c1].bitcast(FP8X4),
                scales=y_scales[:, c0:c1],
                in_=y_grp[:, c0:c1, :].rearrange("p n t -> p (n t)"),
            )

        def store_words(c0, c1, queue=nc.sync):
            queue.dma_start(out=out_words[:, c0:c1], in_=y_codes[:, c0:c1].bitcast(I32))

        def store_scales():
            for q in range(4):
                queue = nc.scalar if q < 3 else nc.sync
                queue.dma_start(
                    out=out_2[0, 4 * q : 4 * q + 4, :].bitcast(I32),
                    in_=y_scales[32 * q : 32 * q + 4, :].bitcast(I32),
                )

        def gate_on_pool(g, c0, c1):
            nc.scalar.copy(out=u_sb[:, g, c0:c1], in_=z[1][g][:, c0:c1])
            nc.gpsimd.tensor_tensor(out=y[:, g, c0:c1], in0=u_sb[:, g, c0:c1], in1=gate[:, g, c0:c1], op=ALU.mult)

        for i in range(2):
            load_x(i)
            load_words(i)
            for g in ORDER:
                load_scales(i, g)

        nc.scalar.activation(out=warm[:], in_=x_scales[:, 0:4].bitcast(F32), func=ACT.Silu)

        interleave_x(0)
        for q in range(2):
            quantise_x(0, q)
        for i in range(2):
            for g in ORDER:
                product(i, g, 0)
        interleave_x(1)
        for q in range(2):
            quantise_x(1, q)
        for g in ORDER:
            silu(g, 0, HALF, HALF)
            gate_bf16(g, 0, HALF, HALF)
            regroup(g, 0, HALF)
        for i, g in ((0, g0), (0, g1), (0, g2), (1, g0), (0, g3), (1, g1), (1, g2), (1, g3)):
            product(i, g, 1)
        third = HALF + QUARTER
        pieces = [(g0, HALF, N), (g1, HALF, N), (g2, HALF, third), (g3, HALF, third), (g2, third, N), (g3, third, N)]
        for g, c0, c1 in pieces:
            silu(g, c0, c1)
            gate_bf16(g, c0, c1)
            regroup(g, c0, c1)
        gate_on_pool(g0, 0, QUARTER)
        gate_on_pool(g2, 0, QUARTER)
        gate_on_pool(g3, 0, HALF)
        for g, c0 in ((g0, QUARTER), (g1, 0), (g2, QUARTER), (g3, HALF)):
            gate_f32(g, c0, N)
            store(g)

        interleave_y(nc.scalar.copy, 0, HALF)
        interleave_y(nc.scalar.copy, HALF, Y_SPLIT)
        interleave_y(nc.vector.tensor_copy, Y_SPLIT, third)
        interleave_y(nc.vector.tensor_copy, third, N)
        quantise_y(0, HALF)
        store_words(0, HALF)
        quantise_y(HALF, third)
        quantise_y(third, N)
        store_words(HALF, N)
        store_scales()
